import numpy as np
import ml_dtypes


def mxq(x, axis, fmt="e4m3"):
    dtype, down = {"e4m3": (ml_dtypes.float8_e4m3fn, 7), "e5m2": (ml_dtypes.float8_e5m2, 14)}[fmt]
    v = np.moveaxis(np.asarray(x, np.float32).astype(ml_dtypes.bfloat16).astype(np.float64), axis, -1)
    blocks = v.reshape(v.shape[:-1] + (-1, 32))
    amax = np.abs(blocks).max(-1, keepdims=True)
    byte = np.maximum(np.where(amax > 0, np.frexp(amax)[1] - 1 + 127, 0) - down, 1)
    scale = np.exp2(byte - 127.0)
    codes = (blocks / scale).astype(np.float32).astype(dtype).astype(np.float64)
    return np.moveaxis((codes * scale).reshape(v.shape), -1, axis)


WIDE = False


def mx_kscale(k):
    if not WIDE:
        return np.ones(k)
    levels = np.array([10, -10, 5, -5, 0])
    if k % 512:
        return np.exp2(np.random.permutation(np.resize(levels, k // 32))).repeat(32)
    a = np.empty((k // 512, 16))
    for p in range(k // 512):
        a[p, :8] = np.random.permutation(np.resize(levels, 8))
        for g in range(8):
            far = levels[np.abs(levels - a[p, g]) >= 10]
            a[p, g + 8] = far[np.random.randint(len(far))]
    return np.exp2(a.ravel()).repeat(32)


def f64(x):
    return np.asarray(x).astype(np.float64)


def striped(idx):
    return np.tile(idx.reshape(-1, 16).T, (8, 1)).astype(np.uint16)


def unstriped(offs):
    return offs[:16].T.reshape(-1).astype(np.int64)


E2M1 = np.array([0.0, 0.5, 1.0, 1.5, 2.0, 3.0, 4.0, 6.0, -0.0, -0.5, -1.0, -1.5, -2.0, -3.0, -4.0, -6.0])


def pack_weight(w, fmt):
    k, n = w.shape
    w = f64(np.asarray(w, np.float32).astype(ml_dtypes.bfloat16)).reshape(k // 32, 32, n)
    amax = np.abs(w).max(1)
    if fmt == "e4m3":
        byte = np.frexp(amax)[1] - 1 + 127 - 7
    else:
        mant, ex = np.frexp(amax / 6.0)
        byte = np.where(mant > 0.5, ex, ex - 1) + 127
    byte = np.clip(np.where(amax > 0, byte, 1), 1, 254)
    scaled = (w * np.exp2(127.0 - byte)[:, None, :]).reshape(k, n).astype(np.float32)
    by_word = np.ascontiguousarray(scaled.reshape(k // 512, 128, 4, n).transpose(0, 1, 3, 2))
    if fmt == "e4m3":
        words = by_word.astype(ml_dtypes.float8_e4m3fn).view(np.uint8)
    else:
        c = by_word.astype(ml_dtypes.float4_e2m1fn).view(np.uint8) & 0xF
        words = (c[..., 0::2] | (c[..., 1::2] << 4)).reshape(k // 512, 128, 2 * n)
    return np.ascontiguousarray(words), np.ascontiguousarray(byte.astype(np.uint8).reshape(k // 512, 16, n))


def unpack_weight(words, scales, fmt):
    g, _, n = scales.shape
    words = np.ascontiguousarray(words).reshape(g, 128, n, -1)
    if fmt == "e4m3":
        vals = words.view(ml_dtypes.float8_e4m3fn).astype(np.float64)
    else:
        nib = np.empty((g, 128, n, 4), np.uint8)
        nib[..., 0::2] = words & 0xF
        nib[..., 1::2] = words >> 4
        vals = E2M1[nib]
    vals = vals * np.repeat(np.exp2(scales.astype(np.float64) - 127.0), 8, axis=1)[..., None]
    return vals.transpose(0, 1, 3, 2).reshape(g * 512, n)


def gelu(v):
    return 0.5 * v * (1.0 + np.tanh(np.sqrt(2.0 / np.pi) * (v + 0.044715 * v**3)))


K, T, S, S2 = 1024, 2048, 512, 1024


def setup_inputs():
    n = np.random.standard_normal
    s = mx_kscale(K)[:, None]
    d = {}
    d["tab_words"], d["tab_scales"] = pack_weight(n((K, T)) * s, "e4m3")
    d["offs"] = striped(np.random.permutation(T)[:S])
    d["offs2"] = striped(np.random.permutation(T)[:S2])
    d["w"] = (n((K, K)) / s / s.T / K).astype(np.float32)
    d["w4_words"], d["w4_scales"] = pack_weight(n((K, K)) / s / K, "e2m1")
    d["gain"] = (np.exp(0.3 * n(K)) / s[:, 0]).astype(np.float32)
    d["pairw"] = n((S2, S)).astype(np.float32)
    return d


def reference(tab_words, tab_scales, offs, offs2, w, w4_words, w4_scales, gain, pairw):
    TW = unpack_weight(tab_words, tab_scales, "e4m3")
    v = TW[:, unstriped(offs)]
    v2 = TW[:, unstriped(offs2)]
    w4 = unpack_weight(w4_words, w4_scales, "e2m1")
    h = np.abs(mxq(f64(w), 0, "e4m3").T @ v)
    b = f64(gain)[:, None] * (w4.T @ v)
    e = v2.T @ mxq(h, 0, "e4m3")
    f = v2.T @ mxq(b, 0, "e4m3")
    return np.tanh(e - f64(pairw) * f)

@@ -1,0 +1,238 @@
+from contextlib import ExitStack
+
+import concourse.mybir as mybir
+
+K, T, S, S2 = 1024, 2048, 512, 1024
+FLOPS = 2 * K * K * S * 2 + 2 * K * S2 * S * 2
+
+F32 = mybir.dt.float32
+BF16 = mybir.dt.bfloat16
+I32 = mybir.dt.int32
+U32 = mybir.dt.uint32
+U16 = mybir.dt.uint16
+U8 = mybir.dt.uint8
+FP8X4 = mybir.dt.float8_e4m3fn_x4
+FP4X4 = mybir.dt.float4_e2m1fn_x4
+ACT = mybir.ActivationFunctionType
+ALU = mybir.AluOpType
+
+P = 128
+PACK = 4
+KP = P * PACK
+NP = K // KP
+BANK = 512
+QUADS = 4
+JH = 256
+
+
+def tile_list_double_bill_carryover_kernel(
+    tc, tab_words, tab_scales, offs, offs2, w, w4_words, w4_scales, gain, pairw, out
+):
+    nc = tc.nc
+    with ExitStack() as ctx:
+        keep = ctx.enter_context(tc.tile_pool(name="keep", bufs=1))
+        ring = ctx.enter_context(tc.tile_pool(name="ring", bufs=8))
+        stream = ctx.enter_context(tc.tile_pool(name="stream", bufs=4))
+        ps1 = ctx.enter_context(tc.psum_pool(name="ps1", bufs=4))
+        ps2 = ctx.enter_context(tc.psum_pool(name="ps2", bufs=4))
+
+        def held(shape, dtype, name):
+            return keep.tile(shape, dtype, name=name, align_bytes=64)
+
+        idx = keep.tile([P, S // 16], U16, name="idx")
+        idx2 = keep.tile([P, S2 // 16], U16, name="idx2")
+        tabw = [held([P, T], I32, "tabw%d" % a) for a in range(NP)]
+        tabs = held([P, T], U8, "tabs")
+        w4w_raw = held([P, NP, 2 * K], U8, "w4w_raw")
+        w4s_raw = held([P, NP * K], U8, "w4s_raw")
+        gains = held([P, NP, PACK], F32, "gains")
+        vs1 = held([P, S], U8, "vs1")
+
+        nc.gpsimd.memset(tabs[:].bitcast(I32), 0)
+        nc.vector.memset(w4s_raw[:].bitcast(I32), 0)
+        nc.gpsimd.memset(vs1[:].bitcast(I32), 0)
+
+        def load_table_words(a, parts):
+            words = tab_words[a].rearrange("p t i -> p (t i)").bitcast(I32)
+            for lo in range(0, T, T // parts):
+                nc.sync.dma_start(out=tabw[a][:, lo : lo + T // parts], in_=words[:, lo : lo + T // parts])
+
+        w_raw = {}
+
+        def load_w(a, b):
+            w_raw[a, b] = stream.tile([P, PACK, KP], F32, name="staged")
+            nc.sync.dma_start(
+                out=w_raw[a, b][:],
+                in_=w[a * KP : (a + 1) * KP, b * KP : (b + 1) * KP].rearrange("(p i) c -> p i c", i=PACK),
+            )
+
+        nc.sync.dma_start(idx[:], offs)
+        load_table_words(0, 2)
+        nc.sync.dma_start(idx2[:], offs2)
+        for q in range(QUADS):
+            nc.sync.dma_start(
+                out=tabs[32 * q : 32 * q + 8, :].bitcast(I32),
+                in_=tab_scales[:, 4 * q : 4 * q + 4, :].bitcast(I32),
+            )
+        nc.sync.dma_start(out=w4w_raw[:].bitcast(I32), in_=w4_words.rearrange("a p c -> p a c").bitcast(I32))
+        load_w(0, 0)
+        for q in range(QUADS):
+            nc.sync.dma_start(
+                out=w4s_raw[32 * q : 32 * q + 4, :].rearrange("r (a c) -> r a c", a=NP).bitcast(I32),
+                in_=w4_scales[:, 4 * q : 4 * q + 4, :].rearrange("a r c -> r a c").bitcast(I32),
+            )
+        nc.sync.dma_start(out=gains[:], in_=gain.rearrange("(b p t) -> p b t", b=NP, t=PACK))
+        load_table_words(1, 1)
+        pw = []
+
+        def load_pairw(g):
+            pw.append(stream.tile([P, PACK, S], F32, name="staged"))
+            nc.sync.dma_start(
+                out=pw[g][:], in_=pairw[g * KP : (g + 1) * KP, :].rearrange("(n p) j -> p n j", p=P)
+            )
+
+        def gather(name, dtype, window, offsets, n):
+            got = held([P, n], dtype, name)
+            nc.vector.tensor_copy(got[:], window.indirect(offsets))
+            return got
+
+        vw = [None, None]
+        vw[0] = gather("vw0", U32, tabw[0][:].bitcast(U32), idx[:], S)
+        vs = gather("vs", U8, tabs[:], idx[:], S)
+        nc.sync.dma_start(out=vs1[0:100, :].bitcast(I32), in_=vs[4:104, :].bitcast(I32))
+        load_w(1, 0)
+        load_w(0, 1)
+        load_w(1, 1)
+        vw[1] = gather("vw1", U32, tabw[1][:].bitcast(U32), idx[:], S)
+
+        w4w = []
+        for a in range(NP):
+            w4w.append(held([P, 2 * K], U8, "w4w%d" % a))
+            nc.scalar.copy(
+                out=w4w[a][:].bitcast(U16).rearrange("p (b t c m) -> p b c t m", b=NP, t=PACK, m=8),
+                in_=w4w_raw[:, a, :].bitcast(U16).rearrange("p (b c m t) -> p b c t m", b=NP, t=PACK, m=8),
+            )
+        w4s = held([P, NP * K], U8, "w4s")
+        nc.vector.tensor_copy(
+            out=w4s[:].rearrange("p (g t c m) -> p g c t m", g=NP * NP, t=PACK, m=16),
+            in_=w4s_raw[:].rearrange("p (g c m t) -> p g c t m", g=NP * NP, t=PACK, m=16),
+        )
+
+        def quantise(name, rounded, width=KP):
+            codes, scales = held([P, width], U32, name + "_codes"), held([P, width], U8, name + "_scales")
+            nc.vector.quantize_mx(out=codes[:].bitcast(FP8X4), scales=scales[:], in_=rounded[:])
+            return codes, scales
+
+        wq = {}
+
+        def quantise_w(a, b):
+            rounded = keep.tile([P, PACK * KP], BF16, name="w_bf", tag="bf%d%d" % (a, b), align_bytes=64)
+            nc.scalar.copy(
+                out=rounded[:].rearrange("p (t m i) -> p m i t", t=PACK, i=PACK),
+                in_=w_raw[a, b][:].rearrange("p i (m t) -> p m i t", t=PACK),
+            )
+            wq[a, b] = quantise("wq%d%d" % (a, b), rounded)
+
+        bq = [None, None]
+
+        def plain_reading(b):
+            by_slot = held([P, PACK, S], BF16, "b_slot%d" % b)
+            for t in range(PACK):
+                rt = PACK * b + t
+                bank = ps1.tile([P, BANK], F32, name="bank1")
+                for a in range(NP):
+                    nc.tensor.matmul_mx(
+                        out=bank[:],
+                        lhsT=w4w[a][:, 2 * P * rt : 2 * P * (rt + 1)].bitcast(FP4X4),
+                        lhsT_scale=w4s[:, a * K + P * rt : a * K + P * (rt + 1)],
+                        rhs=vw[a][:].bitcast(FP8X4),
+                        rhs_scale=(vs if a == 0 else vs1)[:],
+                        start=(a == 0),
+                        stop=(a == NP - 1),
+                    )
+                nc.scalar.activation(out=by_slot[:, t, :], in_=bank[:], func=ACT.Copy, scale=gains[:, b, t : t + 1])
+            rounded = held([P, PACK * S], BF16, "b_bf%d" % b)
+            nc.vector.tensor_copy(
+                out=rounded[:].rearrange("p (c i t) -> p c t i", t=PACK, i=4),
+                in_=by_slot[:].rearrange("p t (c i) -> p c t i", i=4),
+            )
+            bq[b] = quantise("bq%d" % b, rounded)
+
+        hq = {}
+
+        def carry_over(b, jh):
+            rounded = held([P, PACK * JH], BF16, "h_bf%d%d" % (b, jh))
+            for jc in range(JH // P):
+                cols = slice(JH * jh + P * jc, JH * jh + P * (jc + 1))
+                bank = ps1.tile([P, BANK], F32, name="bank1")
+                for t in range(PACK):
+                    for a in range(NP):
+                        nc.tensor.matmul_mx(
+                            out=bank[:, P * t : P * (t + 1)],
+                            lhsT=wq[a, b][0][:, P * t : P * (t + 1)].bitcast(FP8X4),
+                            lhsT_scale=wq[a, b][1][:, P * t : P * (t + 1)],
+                            rhs=vw[a][:, cols].bitcast(FP8X4),
+                            rhs_scale=vs[4 * a : P, cols],
+                            start=(a == 0),
+                            stop=(a == NP - 1),
+                        )
+                nc.scalar.activation(
+                    out=rounded[:, BANK * jc : BANK * (jc + 1)].rearrange("p (j t) -> p j t", t=PACK),
+                    in_=bank[:].rearrange("p (t j) -> p j t", t=PACK),
+                    func=ACT.Abs,
+                )
+            hq[b, jh] = quantise("hq%d%d" % (b, jh), rounded, JH)
+
+        quantise_w(0, 0)
+        plain_reading(0)
+        quantise_w(1, 0)
+        load_pairw(0)
+        load_pairw(1)
+        plain_reading(1)
+
+        v2w = [held([P, S2], U32, "v2w%d" % a) for a in range(NP)]
+        v2s = keep.tile([P, S2], U8, name="v2s", tag="bf10", align_bytes=64)
+        nc.vector.tensor_copy(v2w[0][:], tabw[0][:].bitcast(U32).indirect(idx2[:]))
+        nc.vector.tensor_copy(v2s[:], tabs[:].indirect(idx2[:]))
+        nc.vector.tensor_copy(v2w[1][:], tabw[1][:].bitcast(U32).indirect(idx2[:]))
+
+        quantise_w(0, 1)
+        quantise_w(1, 1)
+        for jh in range(S // JH):
+            for b in range(NP):
+                carry_over(b, jh)
+
+        def match(target, mt, operand):
+            lo = P * mt
+            for b in range(NP):
+                nc.tensor.matmul_mx(
+                    out=target,
+                    lhsT=v2w[b][:, lo : lo + P].bitcast(FP8X4),
+                    lhsT_scale=v2s[4 * b : P, lo : lo + P],
+                    rhs=operand[b][0][:].bitcast(FP8X4),
+                    rhs_scale=operand[b][1][:],
+                    start=(b == 0),
+                    stop=(b == NP - 1),
+                )
+
+        weighted = [held([P, 2, S], F32, "weighted%d" % g) for g in range(S2 // (2 * P))]
+        for mt in range(S2 // P):
+            bank = ps2.tile([P, BANK], F32, name="bank2")
+            match(bank[:], mt, bq)
+            nc.vector.tensor_tensor(
+                weighted[mt // 2][:, mt % 2, :], bank[:], pw[mt // PACK][:, mt % PACK, :], ALU.mult
+            )
+
+        for jh in range(S // JH):
+            cols = slice(JH * jh, JH * (jh + 1))
+            for g in range(S2 // (2 * P)):
+                bank = ps2.tile([P, 2, JH], F32, name="bank2")
+                for n in range(2):
+                    match(bank[:, n, :], 2 * g + n, [hq[b, jh] for b in range(NP)])
+                diff = ring.tile([P, 2, JH], F32, name="diff")
+                nc.vector.tensor_tensor(diff[:], bank[:], weighted[g][:, :, cols], ALU.subtract)
+                score = ring.tile([P, 2, JH], F32, name="score")
+                nc.scalar.activation(out=score[:], in_=diff[:], func=ACT.Tanh)
+                nc.sync.dma_start(
+                    out=out[2 * P * g : 2 * P * (g + 1), cols].rearrange("(n p) j -> p n j", p=P), in_=score[:]
+                )

@@ -23,6 +23,7 @@ NP = K // KP
 BANK = 512
 QUADS = 4
 JH = 256
+PART = 512
 
 
 def tile_list_double_bill_carryover_kernel(
@@ -32,7 +33,8 @@ def tile_list_double_bill_carryover_kernel(
     with ExitStack() as ctx:
         keep = ctx.enter_context(tc.tile_pool(name="keep", bufs=1))
         ring = ctx.enter_context(tc.tile_pool(name="ring", bufs=8))
-        stream = ctx.enter_context(tc.tile_pool(name="stream", bufs=4))
+        stream = ctx.enter_context(tc.tile_pool(name="stream", bufs=6))
+        reuse = ctx.enter_context(tc.tile_pool(name="reuse", bufs=1))
         ps1 = ctx.enter_context(tc.psum_pool(name="ps1", bufs=4))
         ps2 = ctx.enter_context(tc.psum_pool(name="ps2", bufs=4))
 
@@ -44,13 +46,15 @@ def tile_list_double_bill_carryover_kernel(
         tabw = [held([P, T], I32, "tabw%d" % a) for a in range(NP)]
         tabs = held([P, T], U8, "tabs")
         w4w_raw = held([P, NP, 2 * K], U8, "w4w_raw")
-        w4s_raw = held([P, NP * K], U8, "w4s_raw")
+        w4s_raw = reuse.tile([P, K], U8, name="w4s_raw", align_bytes=64, offset=1792)
         gains = held([P, NP, PACK], F32, "gains")
         vs1 = held([P, S], U8, "vs1")
 
         nc.gpsimd.memset(tabs[:].bitcast(I32), 0)
         nc.vector.memset(w4s_raw[:].bitcast(I32), 0)
-        nc.gpsimd.memset(vs1[:].bitcast(I32), 0)
+        w4s1 = held([P, K], U8, "w4s1")
+        nc.vector.memset(w4s1[:].bitcast(I32), 0)
+        nc.vector.memset(vs1[:].bitcast(I32), 0)
 
         def load_table_words(a, parts):
             words = tab_words[a].rearrange("p t i -> p (t i)").bitcast(I32)
@@ -69,20 +73,23 @@ def tile_list_double_bill_carryover_kernel(
         nc.sync.dma_start(idx[:], offs)
         load_table_words(0, 2)
         nc.sync.dma_start(idx2[:], offs2)
+        nc.sync.dma_start(out=gains[:], in_=gain.rearrange("(b p t) -> p b t", b=NP, t=PACK))
         for q in range(QUADS):
-            nc.sync.dma_start(
+            nc.gpsimd.dma_start(
                 out=tabs[32 * q : 32 * q + 8, :].bitcast(I32),
                 in_=tab_scales[:, 4 * q : 4 * q + 4, :].bitcast(I32),
             )
-        nc.sync.dma_start(out=w4w_raw[:].bitcast(I32), in_=w4_words.rearrange("a p c -> p a c").bitcast(I32))
-        load_w(0, 0)
         for q in range(QUADS):
             nc.sync.dma_start(
-                out=w4s_raw[32 * q : 32 * q + 4, :].rearrange("r (a c) -> r a c", a=NP).bitcast(I32),
-                in_=w4_scales[:, 4 * q : 4 * q + 4, :].rearrange("a r c -> r a c").bitcast(I32),
+                out=w4s_raw[32 * q : 32 * q + 8, :].bitcast(I32),
+                in_=w4_scales[:, 4 * q : 4 * q + 4, :].bitcast(I32),
             )
-        nc.sync.dma_start(out=gains[:], in_=gain.rearrange("(b p t) -> p b t", b=NP, t=PACK))
+        nc.sync.dma_start(out=w4w_raw[:].bitcast(I32), in_=w4_words.rearrange("a p c -> p a c").bitcast(I32))
+        load_w(0, 0)
         load_table_words(1, 1)
+        load_w(1, 0)
+        load_w(0, 1)
+        load_w(1, 1)
         pw = []
 
         def load_pairw(g):
@@ -96,13 +103,15 @@ def tile_list_double_bill_carryover_kernel(
             nc.vector.tensor_copy(got[:], window.indirect(offsets))
             return got
 
+        def idx2_part(g):
+            return idx2[:, g * (PART // 16) : (g + 1) * (PART // 16)]
+
         vw = [None, None]
         vw[0] = gather("vw0", U32, tabw[0][:].bitcast(U32), idx[:], S)
         vs = gather("vs", U8, tabs[:], idx[:], S)
-        nc.sync.dma_start(out=vs1[0:100, :].bitcast(I32), in_=vs[4:104, :].bitcast(I32))
-        load_w(1, 0)
-        load_w(0, 1)
-        load_w(1, 1)
+        nc.gpsimd.dma_start(out=vs1[0:100, :].bitcast(I32), in_=vs[4:104, :].bitcast(I32))
+        load_pairw(0)
+        load_pairw(1)
         vw[1] = gather("vw1", U32, tabw[1][:].bitcast(U32), idx[:], S)
 
         w4w = []
@@ -112,11 +121,13 @@ def tile_list_double_bill_carryover_kernel(
                 out=w4w[a][:].bitcast(U16).rearrange("p (b t c m) -> p b c t m", b=NP, t=PACK, m=8),
                 in_=w4w_raw[:, a, :].bitcast(U16).rearrange("p (b c m t) -> p b c t m", b=NP, t=PACK, m=8),
             )
-        w4s = held([P, NP * K], U8, "w4s")
+        w4s = held([P, K], U8, "w4s")
         nc.vector.tensor_copy(
-            out=w4s[:].rearrange("p (g t c m) -> p g c t m", g=NP * NP, t=PACK, m=16),
-            in_=w4s_raw[:].rearrange("p (g c m t) -> p g c t m", g=NP * NP, t=PACK, m=16),
+            out=w4s[:].rearrange("p (g t c m) -> p g c t m", g=NP, t=PACK, m=16),
+            in_=w4s_raw[:].rearrange("p (g c m t) -> p g c t m", g=NP, t=PACK, m=16),
         )
+
+        nc.gpsimd.dma_start(out=w4s1[0:100, :].bitcast(I32), in_=w4s[4:104, :].bitcast(I32))
 
         def quantise(name, rounded, width=KP):
             codes, scales = held([P, width], U32, name + "_codes"), held([P, width], U8, name + "_scales")
@@ -127,7 +138,7 @@ def tile_list_double_bill_carryover_kernel(
 
         def quantise_w(a, b):
             rounded = keep.tile([P, PACK * KP], BF16, name="w_bf", tag="bf%d%d" % (a, b), align_bytes=64)
-            nc.scalar.copy(
+            (nc.vector.tensor_copy if (a, b) in [(1, 0)] else nc.scalar.copy)(
                 out=rounded[:].rearrange("p (t m i) -> p m i t", t=PACK, i=PACK),
                 in_=w_raw[a, b][:].rearrange("p i (m t) -> p m i t", t=PACK),
             )
@@ -136,7 +147,7 @@ def tile_list_double_bill_carryover_kernel(
         bq = [None, None]
 
         def plain_reading(b):
-            by_slot = held([P, PACK, S], BF16, "b_slot%d" % b)
+            by_slot = keep.tile([P, PACK, S], BF16, name="b_slot", tag=["zz","zy"][b], align_bytes=64)
             for t in range(PACK):
                 rt = PACK * b + t
                 bank = ps1.tile([P, BANK], F32, name="bank1")
@@ -144,7 +155,7 @@ def tile_list_double_bill_carryover_kernel(
                     nc.tensor.matmul_mx(
                         out=bank[:],
                         lhsT=w4w[a][:, 2 * P * rt : 2 * P * (rt + 1)].bitcast(FP4X4),
-                        lhsT_scale=w4s[:, a * K + P * rt : a * K + P * (rt + 1)],
+                        lhsT_scale=(w4s if a == 0 else w4s1)[:, P * rt : P * (rt + 1)],
                         rhs=vw[a][:].bitcast(FP8X4),
                         rhs_scale=(vs if a == 0 else vs1)[:],
                         start=(a == 0),
@@ -186,29 +197,31 @@ def tile_list_double_bill_carryover_kernel(
         quantise_w(0, 0)
         plain_reading(0)
         quantise_w(1, 0)
-        load_pairw(0)
-        load_pairw(1)
         plain_reading(1)
-
-        v2w = [held([P, S2], U32, "v2w%d" % a) for a in range(NP)]
-        v2s = keep.tile([P, S2], U8, name="v2s", tag="bf10", align_bytes=64)
-        nc.vector.tensor_copy(v2w[0][:], tabw[0][:].bitcast(U32).indirect(idx2[:]))
-        nc.vector.tensor_copy(v2s[:], tabs[:].indirect(idx2[:]))
-        nc.vector.tensor_copy(v2w[1][:], tabw[1][:].bitcast(U32).indirect(idx2[:]))
+        v2w, v2s = {}, {}
+        v2w[0, 0] = held([P, PART], U32, "v2w00")
+        nc.vector.tensor_copy(v2w[0, 0][:], tabw[0][:].bitcast(U32).indirect(idx2_part(0)))
+        v2w[0, 1] = keep.tile([P, PART], U32, name="v2w01", tag="bf00", align_bytes=64)
+        nc.vector.tensor_copy(v2w[0, 1][:], tabw[0][:].bitcast(U32).indirect(idx2_part(1)))
+        v2s[0] = reuse.tile([P, PART], U8, name="v2s0", align_bytes=64, offset=2048)
+        nc.vector.tensor_copy(v2s[0][:], tabs[:].indirect(idx2_part(0)))
+        v2s[1] = reuse.tile([P, PART], U8, name="v2s1", align_bytes=64, offset=2560)
+        nc.vector.tensor_copy(v2s[1][:], tabs[:].indirect(idx2_part(1)))
+        v2w[1, 0] = reuse.tile([P, PART], U32, name="v2w10", align_bytes=64, offset=0)
+        nc.vector.tensor_copy(v2w[1, 0][:], tabw[1][:].bitcast(U32).indirect(idx2_part(0)))
+        v2w[1, 1] = held([P, PART], U32, "v2w11")
+        nc.vector.tensor_copy(v2w[1, 1][:], tabw[1][:].bitcast(U32).indirect(idx2_part(1)))
 
         quantise_w(0, 1)
         quantise_w(1, 1)
-        for jh in range(S // JH):
-            for b in range(NP):
-                carry_over(b, jh)
 
         def match(target, mt, operand):
-            lo = P * mt
+            g, lo = divmod(P * mt, PART)
             for b in range(NP):
                 nc.tensor.matmul_mx(
                     out=target,
-                    lhsT=v2w[b][:, lo : lo + P].bitcast(FP8X4),
-                    lhsT_scale=v2s[4 * b : P, lo : lo + P],
+                    lhsT=v2w[b, g][:, lo : lo + P].bitcast(FP8X4),
+                    lhsT_scale=v2s[g][4 * b : P, lo : lo + P],
                     rhs=operand[b][0][:].bitcast(FP8X4),
                     rhs_scale=operand[b][1][:],
                     start=(b == 0),
@@ -216,12 +229,20 @@ def tile_list_double_bill_carryover_kernel(
                 )
 
         weighted = [held([P, 2, S], F32, "weighted%d" % g) for g in range(S2 // (2 * P))]
-        for mt in range(S2 // P):
-            bank = ps2.tile([P, BANK], F32, name="bank2")
-            match(bank[:], mt, bq)
-            nc.vector.tensor_tensor(
-                weighted[mt // 2][:, mt % 2, :], bank[:], pw[mt // PACK][:, mt % PACK, :], ALU.mult
-            )
+
+        def weigh(tiles):
+            for mt in tiles:
+                bank = ps2.tile([P, BANK], F32, name="bank2")
+                match(bank[:], mt, bq)
+                nc.vector.tensor_tensor(
+                    weighted[mt // 2][:, mt % 2, :], bank[:], pw[mt // PACK][:, mt % PACK, :], ALU.mult
+                )
+
+        carry_over(0, 0)
+        carry_over(0, 1)
+        carry_over(1, 0)
+        carry_over(1, 1)
+        weigh(range(8))
 
         for jh in range(S // JH):
             cols = slice(JH * jh, JH * (jh + 1))

@@ -1,6 +1,7 @@
 from contextlib import ExitStack
 
 import concourse.mybir as mybir
+from concourse.masks import make_identity
 
 K, T, S, S2 = 1024, 2048, 512, 1024
 FLOPS = 2 * K * K * S * 2 + 2 * K * S2 * S * 2
@@ -24,6 +25,7 @@ BANK = 512
 QUADS = 4
 JH = 256
 PART = 512
+GC = K // P
 
 
 def tile_list_double_bill_carryover_kernel(
@@ -32,142 +34,153 @@ def tile_list_double_bill_carryover_kernel(
     nc = tc.nc
     with ExitStack() as ctx:
         keep = ctx.enter_context(tc.tile_pool(name="keep", bufs=1))
-        ring = ctx.enter_context(tc.tile_pool(name="ring", bufs=8))
-        stream = ctx.enter_context(tc.tile_pool(name="stream", bufs=6))
-        reuse = ctx.enter_context(tc.tile_pool(name="reuse", bufs=1))
+        ring = ctx.enter_context(tc.tile_pool(name="ring", bufs=9))
         ps1 = ctx.enter_context(tc.psum_pool(name="ps1", bufs=4))
         ps2 = ctx.enter_context(tc.psum_pool(name="ps2", bufs=4))
 
-        def held(shape, dtype, name):
-            return keep.tile(shape, dtype, name=name, align_bytes=64)
+        def held(shape, dtype, name, tag=None):
+            return keep.tile(shape, dtype, name=name, tag=tag or name, align_bytes=64)
 
         idx = keep.tile([P, S // 16], U16, name="idx")
         idx2 = keep.tile([P, S2 // 16], U16, name="idx2")
         tabw = [held([P, T], I32, "tabw%d" % a) for a in range(NP)]
         tabs = held([P, T], U8, "tabs")
-        w4w_raw = held([P, NP, 2 * K], U8, "w4w_raw")
-        w4s_raw = reuse.tile([P, K], U8, name="w4s_raw", align_bytes=64, offset=1792)
-        gains = held([P, NP, PACK], F32, "gains")
+        w4w = held([P, NP, 2 * K], U8, "w4w")
+        w4s = held([P, NP * K], U8, "w4s")
+        gain_rows = held([P, GC], F32, "gain_rows")
         vs1 = held([P, S], U8, "vs1")
+        ident = held([P, P], F32, "ident")
 
         nc.gpsimd.memset(tabs[:].bitcast(I32), 0)
-        nc.vector.memset(w4s_raw[:].bitcast(I32), 0)
-        w4s1 = held([P, K], U8, "w4s1")
-        nc.vector.memset(w4s1[:].bitcast(I32), 0)
+        nc.vector.memset(w4s[:].bitcast(I32), 0)
         nc.vector.memset(vs1[:].bitcast(I32), 0)
+        make_identity(nc, ident[:])
 
         def load_table_words(a, parts):
             words = tab_words[a].rearrange("p t i -> p (t i)").bitcast(I32)
             for lo in range(0, T, T // parts):
                 nc.sync.dma_start(out=tabw[a][:, lo : lo + T // parts], in_=words[:, lo : lo + T // parts])
 
+        def load_table_scales():
+            for q in range(QUADS):
+                nc.sync.dma_start(
+                    out=tabs[32 * q : 32 * q + 8, :].bitcast(I32),
+                    in_=tab_scales[:, 4 * q : 4 * q + 4, :].bitcast(I32),
+                )
+
+        def load_w4_scales():
+            for r in range(4):
+                nc.sync.dma_start(
+                    out=w4s[r:P:32, :].rearrange("q (a c) -> q a c", a=NP).bitcast(I32),
+                    in_=w4_scales[:, r:16:4, :].rearrange("a q c -> q a c").bitcast(I32),
+                )
+
         w_raw = {}
 
         def load_w(a, b):
-            w_raw[a, b] = stream.tile([P, PACK, KP], F32, name="staged")
+            w_raw[a, b] = held([P, PACK, KP], F32, "w_raw%d%d" % (a, b))
             nc.sync.dma_start(
                 out=w_raw[a, b][:],
                 in_=w[a * KP : (a + 1) * KP, b * KP : (b + 1) * KP].rearrange("(p i) c -> p i c", i=PACK),
             )
 
-        nc.sync.dma_start(idx[:], offs)
-        load_table_words(0, 2)
-        nc.sync.dma_start(idx2[:], offs2)
-        nc.sync.dma_start(out=gains[:], in_=gain.rearrange("(b p t) -> p b t", b=NP, t=PACK))
-        for q in range(QUADS):
-            nc.gpsimd.dma_start(
-                out=tabs[32 * q : 32 * q + 8, :].bitcast(I32),
-                in_=tab_scales[:, 4 * q : 4 * q + 4, :].bitcast(I32),
-            )
-        for q in range(QUADS):
-            nc.sync.dma_start(
-                out=w4s_raw[32 * q : 32 * q + 8, :].bitcast(I32),
-                in_=w4_scales[:, 4 * q : 4 * q + 4, :].bitcast(I32),
-            )
-        nc.sync.dma_start(out=w4w_raw[:].bitcast(I32), in_=w4_words.rearrange("a p c -> p a c").bitcast(I32))
-        load_w(0, 0)
-        load_table_words(1, 1)
-        load_w(1, 0)
-        load_w(0, 1)
-        load_w(1, 1)
         pw = []
 
         def load_pairw(g):
-            pw.append(stream.tile([P, PACK, S], F32, name="staged"))
+            pw.append(held([P, PACK, S], F32, "pw%d" % g))
             nc.sync.dma_start(
                 out=pw[g][:], in_=pairw[g * KP : (g + 1) * KP, :].rearrange("(n p) j -> p n j", p=P)
             )
 
-        def gather(name, dtype, window, offsets, n):
-            got = held([P, n], dtype, name)
+        def gather(name, dtype, window, offsets, tag=None):
+            got = held([P, PART], dtype, name, tag)
             nc.vector.tensor_copy(got[:], window.indirect(offsets))
             return got
 
         def idx2_part(g):
             return idx2[:, g * (PART // 16) : (g + 1) * (PART // 16)]
 
+        nc.sync.dma_start(idx[:], offs)
+        load_table_words(0, 2)
+        nc.sync.dma_start(out=gain_rows[:], in_=gain.rearrange("(p c) -> p c", c=GC))
+        load_table_scales()
+        nc.sync.dma_start(idx2[:], offs2)
+        nc.sync.dma_start(out=w4w[:].bitcast(I32), in_=w4_words.rearrange("a p c -> p a c").bitcast(I32))
+        load_table_words(1, 1)
+        load_w4_scales()
+
         vw = [None, None]
-        vw[0] = gather("vw0", U32, tabw[0][:].bitcast(U32), idx[:], S)
-        vs = gather("vs", U8, tabs[:], idx[:], S)
-        nc.gpsimd.dma_start(out=vs1[0:100, :].bitcast(I32), in_=vs[4:104, :].bitcast(I32))
+        vw[0] = gather("vw0", U32, tabw[0][:].bitcast(U32), idx[:])
+        vs = gather("vs", U8, tabs[:], idx[:])
+        nc.sync.dma_start(out=vs1[0:100, :].bitcast(I32), in_=vs[4:104, :].bitcast(I32))
+        load_w(0, 0)
+        load_w(1, 0)
+        load_w(0, 1)
+        load_w(1, 1)
         load_pairw(0)
         load_pairw(1)
-        vw[1] = gather("vw1", U32, tabw[1][:].bitcast(U32), idx[:], S)
 
-        w4w = []
-        for a in range(NP):
-            w4w.append(held([P, 2 * K], U8, "w4w%d" % a))
+        vw[1] = gather("vw1", U32, tabw[1][:].bitcast(U32), idx[:])
+
+        gain_all = held([P, K], F32, "gain_all")
+        for half in range(GC // PACK):
+            bank = ps2.tile([P, PACK, P], F32, name="bank2")
+            for c in range(PACK):
+                col = PACK * half + c
+                nc.tensor.transpose(bank[:, c, :], gain_rows[:, col : col + 1].to_broadcast([P, P]), ident[:])
             nc.scalar.copy(
-                out=w4w[a][:].bitcast(U16).rearrange("p (b t c m) -> p b c t m", b=NP, t=PACK, m=8),
-                in_=w4w_raw[:, a, :].bitcast(U16).rearrange("p (b c m t) -> p b c t m", b=NP, t=PACK, m=8),
+                out=gain_all[:].rearrange("q (n h c) -> q h n c", h=GC // PACK, c=PACK)[:, half],
+                in_=bank[:].rearrange("q c n -> q n c"),
             )
-        w4s = held([P, K], U8, "w4s")
-        nc.vector.tensor_copy(
-            out=w4s[:].rearrange("p (g t c m) -> p g c t m", g=NP, t=PACK, m=16),
-            in_=w4s_raw[:].rearrange("p (g c m t) -> p g c t m", g=NP, t=PACK, m=16),
-        )
 
-        nc.gpsimd.dma_start(out=w4s1[0:100, :].bitcast(I32), in_=w4s[4:104, :].bitcast(I32))
-
-        def quantise(name, rounded, width=KP):
+        def quantise(name, rounded, width):
             codes, scales = held([P, width], U32, name + "_codes"), held([P, width], U8, name + "_scales")
             nc.vector.quantize_mx(out=codes[:].bitcast(FP8X4), scales=scales[:], in_=rounded[:])
             return codes, scales
 
         wq = {}
 
-        def quantise_w(a, b):
-            rounded = keep.tile([P, PACK * KP], BF16, name="w_bf", tag="bf%d%d" % (a, b), align_bytes=64)
-            (nc.vector.tensor_copy if (a, b) in [(1, 0)] else nc.scalar.copy)(
+        def quantise_w(a, b, tag=None):
+            rounded = held([P, PACK * KP], BF16, "w_bf%d%d" % (a, b), tag)
+            nc.scalar.copy(
                 out=rounded[:].rearrange("p (t m i) -> p m i t", t=PACK, i=PACK),
                 in_=w_raw[a, b][:].rearrange("p i (m t) -> p m i t", t=PACK),
             )
-            wq[a, b] = quantise("wq%d%d" % (a, b), rounded)
+            wq[a, b] = quantise("wq%d%d" % (a, b), rounded, KP)
 
         bq = [None, None]
 
         def plain_reading(b):
-            by_slot = keep.tile([P, PACK, S], BF16, name="b_slot", tag=["zz","zy"][b], align_bytes=64)
-            for t in range(PACK):
-                rt = PACK * b + t
+            rows = []
+            for jt in range(S // P):
+                cols = slice(P * jt, P * (jt + 1))
                 bank = ps1.tile([P, BANK], F32, name="bank1")
                 for a in range(NP):
                     nc.tensor.matmul_mx(
                         out=bank[:],
-                        lhsT=w4w[a][:, 2 * P * rt : 2 * P * (rt + 1)].bitcast(FP4X4),
-                        lhsT_scale=(w4s if a == 0 else w4s1)[:, P * rt : P * (rt + 1)],
-                        rhs=vw[a][:].bitcast(FP8X4),
-                        rhs_scale=(vs if a == 0 else vs1)[:],
+                        lhsT=vw[a][:, cols].bitcast(FP8X4),
+                        lhsT_scale=(vs if a == 0 else vs1)[:, cols],
+                        rhs=w4w[:, a, 2 * KP * b : 2 * KP * (b + 1)].bitcast(FP4X4),
+                        rhs_scale=w4s[:, K * a + KP * b : K * a + KP * (b + 1)],
                         start=(a == 0),
                         stop=(a == NP - 1),
                     )
-                nc.scalar.activation(out=by_slot[:, t, :], in_=bank[:], func=ACT.Copy, scale=gains[:, b, t : t + 1])
+                rows.append(held([P, KP], BF16, "b_rows%d%d" % (b, jt)))
+                nc.vector.tensor_tensor(rows[jt][:], bank[:], gain_all[:, KP * b : KP * (b + 1)], ALU.mult)
             rounded = held([P, PACK * S], BF16, "b_bf%d" % b)
-            nc.vector.tensor_copy(
-                out=rounded[:].rearrange("p (c i t) -> p c t i", t=PACK, i=4),
-                in_=by_slot[:].rearrange("p t (c i) -> p c t i", i=4),
-            )
-            bq[b] = quantise("bq%d" % b, rounded)
+            for pair in range(S // (2 * P)):
+                bank = ps2.tile([P, 2, 2, P], F32, name="bank2")
+                for n in range(2):
+                    words = rows[2 * pair + n][:].bitcast(F32)
+                    for u in range(2):
+                        nc.tensor.transpose(bank[:, n, u, :], words[:, u : KP // 2 : 2], ident[:])
+                nc.scalar.copy(
+                    out=rounded[:].bitcast(F32)[:, BANK * pair : BANK * (pair + 1)].rearrange(
+                        "p (n j u) -> p n j u", n=2, u=2
+                    ),
+                    in_=bank[:].rearrange("p n u j -> p n j u"),
+                )
+            bq[b] = quantise("bq%d" % b, rounded, S)
 
         hq = {}
 
@@ -194,26 +207,13 @@ def tile_list_double_bill_carryover_kernel(
                 )
             hq[b, jh] = quantise("hq%d%d" % (b, jh), rounded, JH)
 
-        quantise_w(0, 0)
-        plain_reading(0)
-        quantise_w(1, 0)
-        plain_reading(1)
         v2w, v2s = {}, {}
-        v2w[0, 0] = held([P, PART], U32, "v2w00")
-        nc.vector.tensor_copy(v2w[0, 0][:], tabw[0][:].bitcast(U32).indirect(idx2_part(0)))
-        v2w[0, 1] = keep.tile([P, PART], U32, name="v2w01", tag="bf00", align_bytes=64)
-        nc.vector.tensor_copy(v2w[0, 1][:], tabw[0][:].bitcast(U32).indirect(idx2_part(1)))
-        v2s[0] = reuse.tile([P, PART], U8, name="v2s0", align_bytes=64, offset=2048)
-        nc.vector.tensor_copy(v2s[0][:], tabs[:].indirect(idx2_part(0)))
-        v2s[1] = reuse.tile([P, PART], U8, name="v2s1", align_bytes=64, offset=2560)
-        nc.vector.tensor_copy(v2s[1][:], tabs[:].indirect(idx2_part(1)))
-        v2w[1, 0] = reuse.tile([P, PART], U32, name="v2w10", align_bytes=64, offset=0)
-        nc.vector.tensor_copy(v2w[1, 0][:], tabw[1][:].bitcast(U32).indirect(idx2_part(0)))
-        v2w[1, 1] = held([P, PART], U32, "v2w11")
-        nc.vector.tensor_copy(v2w[1, 1][:], tabw[1][:].bitcast(U32).indirect(idx2_part(1)))
 
-        quantise_w(0, 1)
-        quantise_w(1, 1)
+        def gather_opening_words(a, g, tag=None):
+            v2w[a, g] = gather("v2w%d%d" % (a, g), U32, tabw[a][:].bitcast(U32), idx2_part(g), tag)
+
+        def gather_opening_scales(g, tag=None):
+            v2s[g] = gather("v2s%d" % g, U8, tabs[:], idx2_part(g), tag)
 
         def match(target, mt, operand):
             g, lo = divmod(P * mt, PART)
@@ -238,6 +238,18 @@ def tile_list_double_bill_carryover_kernel(
                     weighted[mt // 2][:, mt % 2, :], bank[:], pw[mt // PACK][:, mt % PACK, :], ALU.mult
                 )
 
+        quantise_w(0, 0)
+        plain_reading(0)
+        plain_reading(1)
+        quantise_w(1, 0)
+        gather_opening_words(0, 0)
+        gather_opening_words(0, 1)
+        gather_opening_scales(0, "b_rows10")
+        gather_opening_scales(1, "b_rows11")
+        gather_opening_words(1, 0)
+        gather_opening_words(1, 1, "b_rows12")
+        quantise_w(0, 1)
+        quantise_w(1, 1)
         carry_over(0, 0)
         carry_over(0, 1)
         carry_over(1, 0)
@@ -250,10 +262,13 @@ def tile_list_double_bill_carryover_kernel(
                 bank = ps2.tile([P, 2, JH], F32, name="bank2")
                 for n in range(2):
                     match(bank[:, n, :], 2 * g + n, [hq[b, jh] for b in range(NP)])
-                diff = ring.tile([P, 2, JH], F32, name="diff")
-                nc.vector.tensor_tensor(diff[:], bank[:], weighted[g][:, :, cols], ALU.subtract)
-                score = ring.tile([P, 2, JH], F32, name="score")
-                nc.scalar.activation(out=score[:], in_=diff[:], func=ACT.Tanh)
-                nc.sync.dma_start(
-                    out=out[2 * P * g : 2 * P * (g + 1), cols].rearrange("(n p) j -> p n j", p=P), in_=score[:]
-                )
+                last = jh == S // JH - 1 and g == S2 // (2 * P) - 1
+                step = 1 if last else 2
+                for lo in range(0, 2, step):
+                    tiles = slice(lo, lo + step)
+                    diff = ring.tile([P, step, JH], F32, name="diff")
+                    nc.vector.tensor_tensor(diff[:], bank[:, tiles, :], weighted[g][:, tiles, cols], ALU.subtract)
+                    score = ring.tile([P, step, JH], F32, name="score")
+                    nc.scalar.activation(out=score[:], in_=diff[:], func=ACT.Tanh)
+                    rows = slice(P * (2 * g + lo), P * (2 * g + lo + step))
+                    nc.sync.dma_start(out=out[rows, cols].rearrange("(n p) j -> p n j", p=P), in_=score[:])

@@ -87,10 +87,11 @@ def tile_list_double_bill_carryover_kernel(
         pw = []
 
         def load_pairw(g):
-            pw.append(held([P, PACK, S], F32, "pw%d" % g))
-            nc.sync.dma_start(
-                out=pw[g][:], in_=pairw[g * KP : (g + 1) * KP, :].rearrange("(n p) j -> p n j", p=P)
-            )
+            for g2 in (2 * g, 2 * g + 1):
+                pw.append(held([P, 2, S], F32, "pw%d" % g2))
+                nc.sync.dma_start(
+                    out=pw[g2][:], in_=pairw[g2 * 2 * P : (g2 + 1) * 2 * P, :].rearrange("(n p) j -> p n j", p=P)
+                )
 
         def gather(name, dtype, window, offsets, tag=None):
             got = held([P, PART], dtype, name, tag)
@@ -142,10 +143,12 @@ def tile_list_double_bill_carryover_kernel(
 
         def quantise_w(a, b, tag=None):
             rounded = held([P, PACK * KP], BF16, "w_bf%d%d" % (a, b), tag)
-            nc.scalar.copy(
-                out=rounded[:].rearrange("p (t m i) -> p m i t", t=PACK, i=PACK),
-                in_=w_raw[a, b][:].rearrange("p i (m t) -> p m i t", t=PACK),
-            )
+            dst = rounded[:].rearrange("p (t m i) -> p m i t", t=PACK, i=PACK)
+            src = w_raw[a, b][:].rearrange("p i (m t) -> p m i t", t=PACK)
+            cut = 64 if (a, b) in [(1, 1)] else P
+            nc.scalar.copy(out=dst[:, :cut], in_=src[:, :cut])
+            if cut < P:
+                nc.vector.tensor_copy(out=dst[:, cut:], in_=src[:, cut:])
             wq[a, b] = quantise("wq%d%d" % (a, b), rounded, KP)
 
         bq = [None, None]
@@ -235,7 +238,7 @@ def tile_list_double_bill_carryover_kernel(
                 bank = ps2.tile([P, BANK], F32, name="bank2")
                 match(bank[:], mt, bq)
                 nc.vector.tensor_tensor(
-                    weighted[mt // 2][:, mt % 2, :], bank[:], pw[mt // PACK][:, mt % PACK, :], ALU.mult
+                    weighted[mt // 2][:, mt % 2, :], bank[:], pw[mt // 2][:, mt % 2, :], ALU.mult
                 )
 
         quantise_w(0, 0)
@@ -243,18 +246,19 @@ def tile_list_double_bill_carryover_kernel(
         plain_reading(1)
         quantise_w(1, 0)
         gather_opening_words(0, 0)
-        gather_opening_words(0, 1)
-        gather_opening_scales(0, "b_rows10")
-        gather_opening_scales(1, "b_rows11")
+        gather_opening_scales(0)
         gather_opening_words(1, 0)
+        gather_opening_words(0, 1)
+        gather_opening_scales(1, "w_bf10")
         gather_opening_words(1, 1, "b_rows12")
         quantise_w(0, 1)
         quantise_w(1, 1)
+        weigh(range(4))
         carry_over(0, 0)
         carry_over(0, 1)
         carry_over(1, 0)
         carry_over(1, 1)
-        weigh(range(8))
+        weigh(range(4, 8))
 
         for jh in range(S // JH):
             cols = slice(JH * jh, JH * (jh + 1))

@@ -23,9 +23,14 @@ KP = P * PACK
 NP = K // KP
 BANK = 512
 QUADS = 4
-JH = 256
+SCALE_ROWS = 4
+LIST_GROUP = 16
 PART = 512
-GC = K // P
+JH = S // 2
+PAIR = 2
+GAIN_RUN = K // P
+LAST_QUARTER_CUT = P // 2
+EPILOGUE_STEPS = (S // JH) * (S2 // (PAIR * P)) + 1
 
 
 def tile_list_double_bill_carryover_kernel(
@@ -34,20 +39,20 @@ def tile_list_double_bill_carryover_kernel(
     nc = tc.nc
     with ExitStack() as ctx:
         keep = ctx.enter_context(tc.tile_pool(name="keep", bufs=1))
-        ring = ctx.enter_context(tc.tile_pool(name="ring", bufs=9))
+        ring = ctx.enter_context(tc.tile_pool(name="ring", bufs=EPILOGUE_STEPS))
         ps1 = ctx.enter_context(tc.psum_pool(name="ps1", bufs=4))
         ps2 = ctx.enter_context(tc.psum_pool(name="ps2", bufs=4))
 
         def held(shape, dtype, name, tag=None):
             return keep.tile(shape, dtype, name=name, tag=tag or name, align_bytes=64)
 
-        idx = keep.tile([P, S // 16], U16, name="idx")
-        idx2 = keep.tile([P, S2 // 16], U16, name="idx2")
+        idx = keep.tile([P, S // LIST_GROUP], U16, name="idx")
+        idx2 = keep.tile([P, S2 // LIST_GROUP], U16, name="idx2")
         tabw = [held([P, T], I32, "tabw%d" % a) for a in range(NP)]
         tabs = held([P, T], U8, "tabs")
         w4w = held([P, NP, 2 * K], U8, "w4w")
         w4s = held([P, NP * K], U8, "w4s")
-        gain_rows = held([P, GC], F32, "gain_rows")
+        gain_rows = held([P, GAIN_RUN], F32, "gain_rows")
         vs1 = held([P, S], U8, "vs1")
         ident = held([P, P], F32, "ident")
 
@@ -56,54 +61,51 @@ def tile_list_double_bill_carryover_kernel(
         nc.vector.memset(vs1[:].bitcast(I32), 0)
         make_identity(nc, ident[:])
 
-        def load_table_words(a, parts):
+        def load_table_words(a, pieces):
             words = tab_words[a].rearrange("p t i -> p (t i)").bitcast(I32)
-            for lo in range(0, T, T // parts):
-                nc.sync.dma_start(out=tabw[a][:, lo : lo + T // parts], in_=words[:, lo : lo + T // parts])
+            for lo in range(0, T, T // pieces):
+                nc.sync.dma_start(out=tabw[a][:, lo : lo + T // pieces], in_=words[:, lo : lo + T // pieces])
 
         def load_table_scales():
             for q in range(QUADS):
                 nc.sync.dma_start(
-                    out=tabs[32 * q : 32 * q + 8, :].bitcast(I32),
-                    in_=tab_scales[:, 4 * q : 4 * q + 4, :].bitcast(I32),
+                    out=tabs[32 * q : 32 * q + NP * SCALE_ROWS, :].bitcast(I32),
+                    in_=tab_scales[:, SCALE_ROWS * q : SCALE_ROWS * (q + 1), :].bitcast(I32),
                 )
 
         def load_w4_scales():
-            for r in range(4):
+            for s in range(SCALE_ROWS):
                 nc.sync.dma_start(
-                    out=w4s[r:P:32, :].rearrange("q (a c) -> q a c", a=NP).bitcast(I32),
-                    in_=w4_scales[:, r:16:4, :].rearrange("a q c -> q a c").bitcast(I32),
+                    out=w4s[s:P:32, :].rearrange("q (a c) -> q a c", a=NP).bitcast(I32),
+                    in_=w4_scales[:, s : QUADS * SCALE_ROWS : SCALE_ROWS, :].rearrange("a q c -> q a c").bitcast(I32),
                 )
 
         w_raw = {}
 
-        def load_w(a, b):
-            w_raw[a, b] = held([P, PACK, KP], F32, "w_raw%d%d" % (a, b))
+        def load_w(a, rp):
+            w_raw[a, rp] = held([P, PACK, KP], F32, "w_raw%d%d" % (a, rp))
             nc.sync.dma_start(
-                out=w_raw[a, b][:],
-                in_=w[a * KP : (a + 1) * KP, b * KP : (b + 1) * KP].rearrange("(p i) c -> p i c", i=PACK),
+                out=w_raw[a, rp][:],
+                in_=w[a * KP : (a + 1) * KP, rp * KP : (rp + 1) * KP].rearrange("(p i) c -> p i c", i=PACK),
             )
 
         pw = []
 
-        def load_pairw(g):
-            for g2 in (2 * g, 2 * g + 1):
-                pw.append(held([P, 2, S], F32, "pw%d" % g2))
-                nc.sync.dma_start(
-                    out=pw[g2][:], in_=pairw[g2 * 2 * P : (g2 + 1) * 2 * P, :].rearrange("(n p) j -> p n j", p=P)
-                )
+        def load_pairw(pair):
+            pw.append(held([P, PAIR, S], F32, "pw%d" % pair))
+            nc.sync.dma_start(
+                out=pw[pair][:],
+                in_=pairw[pair * PAIR * P : (pair + 1) * PAIR * P, :].rearrange("(n p) j -> p n j", p=P),
+            )
 
         def gather(name, dtype, window, offsets, tag=None):
             got = held([P, PART], dtype, name, tag)
             nc.vector.tensor_copy(got[:], window.indirect(offsets))
             return got
 
-        def idx2_part(g):
-            return idx2[:, g * (PART // 16) : (g + 1) * (PART // 16)]
-
         nc.sync.dma_start(idx[:], offs)
         load_table_words(0, 2)
-        nc.sync.dma_start(out=gain_rows[:], in_=gain.rearrange("(p c) -> p c", c=GC))
+        nc.sync.dma_start(out=gain_rows[:], in_=gain.rearrange("(p c) -> p c", c=GAIN_RUN))
         load_table_scales()
         nc.sync.dma_start(idx2[:], offs2)
         nc.sync.dma_start(out=w4w[:].bitcast(I32), in_=w4_words.rearrange("a p c -> p a c").bitcast(I32))
@@ -113,24 +115,24 @@ def tile_list_double_bill_carryover_kernel(
         vw = [None, None]
         vw[0] = gather("vw0", U32, tabw[0][:].bitcast(U32), idx[:])
         vs = gather("vs", U8, tabs[:], idx[:])
-        nc.sync.dma_start(out=vs1[0:100, :].bitcast(I32), in_=vs[4:104, :].bitcast(I32))
-        load_w(0, 0)
-        load_w(1, 0)
-        load_w(0, 1)
-        load_w(1, 1)
-        load_pairw(0)
-        load_pairw(1)
+        span = 32 * (QUADS - 1) + SCALE_ROWS
+        nc.sync.dma_start(out=vs1[0:span, :].bitcast(I32), in_=vs[SCALE_ROWS : SCALE_ROWS + span, :].bitcast(I32))
+        for rp in range(NP):
+            for a in range(NP):
+                load_w(a, rp)
+        for pair in range(S2 // (PAIR * P)):
+            load_pairw(pair)
 
         vw[1] = gather("vw1", U32, tabw[1][:].bitcast(U32), idx[:])
 
         gain_all = held([P, K], F32, "gain_all")
-        for half in range(GC // PACK):
+        for run in range(GAIN_RUN // PACK):
             bank = ps2.tile([P, PACK, P], F32, name="bank2")
             for c in range(PACK):
-                col = PACK * half + c
+                col = PACK * run + c
                 nc.tensor.transpose(bank[:, c, :], gain_rows[:, col : col + 1].to_broadcast([P, P]), ident[:])
             nc.scalar.copy(
-                out=gain_all[:].rearrange("q (n h c) -> q h n c", h=GC // PACK, c=PACK)[:, half],
+                out=gain_all[:].rearrange("q (n h c) -> q h n c", h=GAIN_RUN // PACK, c=PACK)[:, run],
                 in_=bank[:].rearrange("q c n -> q n c"),
             )
 
@@ -141,138 +143,131 @@ def tile_list_double_bill_carryover_kernel(
 
         wq = {}
 
-        def quantise_w(a, b, tag=None):
-            rounded = held([P, PACK * KP], BF16, "w_bf%d%d" % (a, b), tag)
+        def quantise_w(a, rp, cut=P):
+            rounded = held([P, PACK * KP], BF16, "w_bf%d%d" % (a, rp))
             dst = rounded[:].rearrange("p (t m i) -> p m i t", t=PACK, i=PACK)
-            src = w_raw[a, b][:].rearrange("p i (m t) -> p m i t", t=PACK)
-            cut = 64 if (a, b) in [(1, 1)] else P
+            src = w_raw[a, rp][:].rearrange("p i (m t) -> p m i t", t=PACK)
             nc.scalar.copy(out=dst[:, :cut], in_=src[:, :cut])
             if cut < P:
                 nc.vector.tensor_copy(out=dst[:, cut:], in_=src[:, cut:])
-            wq[a, b] = quantise("wq%d%d" % (a, b), rounded, KP)
+            wq[a, rp] = quantise("wq%d%d" % (a, rp), rounded, KP)
 
         bq = [None, None]
 
-        def plain_reading(b):
-            rows = []
+        def plain_reading(rp):
+            b_rows = []
             for jt in range(S // P):
-                cols = slice(P * jt, P * (jt + 1))
+                jcols = slice(P * jt, P * (jt + 1))
                 bank = ps1.tile([P, BANK], F32, name="bank1")
                 for a in range(NP):
                     nc.tensor.matmul_mx(
                         out=bank[:],
-                        lhsT=vw[a][:, cols].bitcast(FP8X4),
-                        lhsT_scale=(vs if a == 0 else vs1)[:, cols],
-                        rhs=w4w[:, a, 2 * KP * b : 2 * KP * (b + 1)].bitcast(FP4X4),
-                        rhs_scale=w4s[:, K * a + KP * b : K * a + KP * (b + 1)],
+                        lhsT=vw[a][:, jcols].bitcast(FP8X4),
+                        lhsT_scale=(vs if a == 0 else vs1)[:, jcols],
+                        rhs=w4w[:, a, 2 * KP * rp : 2 * KP * (rp + 1)].bitcast(FP4X4),
+                        rhs_scale=w4s[:, K * a + KP * rp : K * a + KP * (rp + 1)],
                         start=(a == 0),
                         stop=(a == NP - 1),
                     )
-                rows.append(held([P, KP], BF16, "b_rows%d%d" % (b, jt)))
-                nc.vector.tensor_tensor(rows[jt][:], bank[:], gain_all[:, KP * b : KP * (b + 1)], ALU.mult)
-            rounded = held([P, PACK * S], BF16, "b_bf%d" % b)
-            for pair in range(S // (2 * P)):
+                b_rows.append(held([P, KP], BF16, "b_rows%d%d" % (rp, jt)))
+                nc.vector.tensor_tensor(b_rows[jt][:], bank[:], gain_all[:, KP * rp : KP * (rp + 1)], ALU.mult)
+            rounded = held([P, PACK * S], BF16, "b_bf%d" % rp)
+            for two in range(S // (2 * P)):
                 bank = ps2.tile([P, 2, 2, P], F32, name="bank2")
                 for n in range(2):
-                    words = rows[2 * pair + n][:].bitcast(F32)
+                    words = b_rows[2 * two + n][:].bitcast(F32)
                     for u in range(2):
                         nc.tensor.transpose(bank[:, n, u, :], words[:, u : KP // 2 : 2], ident[:])
                 nc.scalar.copy(
-                    out=rounded[:].bitcast(F32)[:, BANK * pair : BANK * (pair + 1)].rearrange(
+                    out=rounded[:].bitcast(F32)[:, BANK * two : BANK * (two + 1)].rearrange(
                         "p (n j u) -> p n j u", n=2, u=2
                     ),
                     in_=bank[:].rearrange("p n u j -> p n j u"),
                 )
-            bq[b] = quantise("bq%d" % b, rounded, S)
+            bq[rp] = quantise("bq%d" % rp, rounded, S)
 
         hq = {}
 
-        def carry_over(b, jh):
-            rounded = held([P, PACK * JH], BF16, "h_bf%d%d" % (b, jh))
-            for jc in range(JH // P):
-                cols = slice(JH * jh + P * jc, JH * jh + P * (jc + 1))
+        def carry_over(rp, jh):
+            rounded = held([P, PACK * JH], BF16, "h_bf%d%d" % (rp, jh))
+            for jt in range(JH // P):
+                jcols = slice(JH * jh + P * jt, JH * jh + P * (jt + 1))
                 bank = ps1.tile([P, BANK], F32, name="bank1")
                 for t in range(PACK):
                     for a in range(NP):
                         nc.tensor.matmul_mx(
                             out=bank[:, P * t : P * (t + 1)],
-                            lhsT=wq[a, b][0][:, P * t : P * (t + 1)].bitcast(FP8X4),
-                            lhsT_scale=wq[a, b][1][:, P * t : P * (t + 1)],
-                            rhs=vw[a][:, cols].bitcast(FP8X4),
-                            rhs_scale=vs[4 * a : P, cols],
+                            lhsT=wq[a, rp][0][:, P * t : P * (t + 1)].bitcast(FP8X4),
+                            lhsT_scale=wq[a, rp][1][:, P * t : P * (t + 1)],
+                            rhs=vw[a][:, jcols].bitcast(FP8X4),
+                            rhs_scale=vs[SCALE_ROWS * a : P, jcols],
                             start=(a == 0),
                             stop=(a == NP - 1),
                         )
                 nc.scalar.activation(
-                    out=rounded[:, BANK * jc : BANK * (jc + 1)].rearrange("p (j t) -> p j t", t=PACK),
+                    out=rounded[:, BANK * jt : BANK * (jt + 1)].rearrange("p (j t) -> p j t", t=PACK),
                     in_=bank[:].rearrange("p (t j) -> p j t", t=PACK),
                     func=ACT.Abs,
                 )
-            hq[b, jh] = quantise("hq%d%d" % (b, jh), rounded, JH)
+            hq[rp, jh] = quantise("hq%d%d" % (rp, jh), rounded, JH)
 
         v2w, v2s = {}, {}
 
-        def gather_opening_words(a, g, tag=None):
-            v2w[a, g] = gather("v2w%d%d" % (a, g), U32, tabw[a][:].bitcast(U32), idx2_part(g), tag)
-
-        def gather_opening_scales(g, tag=None):
-            v2s[g] = gather("v2s%d" % g, U8, tabs[:], idx2_part(g), tag)
+        def gather_opening(part, scales_tag=None, last_words_tag=None):
+            offsets = idx2[:, part * (PART // LIST_GROUP) : (part + 1) * (PART // LIST_GROUP)]
+            v2w[0, part] = gather("v2w0%d" % part, U32, tabw[0][:].bitcast(U32), offsets)
+            v2s[part] = gather("v2s%d" % part, U8, tabs[:], offsets, scales_tag)
+            v2w[1, part] = gather("v2w1%d" % part, U32, tabw[1][:].bitcast(U32), offsets, last_words_tag)
 
         def match(target, mt, operand):
-            g, lo = divmod(P * mt, PART)
-            for b in range(NP):
+            part, lo = divmod(P * mt, PART)
+            for rp in range(NP):
                 nc.tensor.matmul_mx(
                     out=target,
-                    lhsT=v2w[b, g][:, lo : lo + P].bitcast(FP8X4),
-                    lhsT_scale=v2s[g][4 * b : P, lo : lo + P],
-                    rhs=operand[b][0][:].bitcast(FP8X4),
-                    rhs_scale=operand[b][1][:],
-                    start=(b == 0),
-                    stop=(b == NP - 1),
+                    lhsT=v2w[rp, part][:, lo : lo + P].bitcast(FP8X4),
+                    lhsT_scale=v2s[part][SCALE_ROWS * rp : P, lo : lo + P],
+                    rhs=operand[rp][0][:].bitcast(FP8X4),
+                    rhs_scale=operand[rp][1][:],
+                    start=(rp == 0),
+                    stop=(rp == NP - 1),
                 )
 
-        weighted = [held([P, 2, S], F32, "weighted%d" % g) for g in range(S2 // (2 * P))]
+        weighted = [held([P, PAIR, S], F32, "weighted%d" % pair) for pair in range(S2 // (PAIR * P))]
 
-        def weigh(tiles):
-            for mt in tiles:
+        def weigh(part):
+            for mt in range(part * PART // P, (part + 1) * PART // P):
+                pair, n = divmod(mt, PAIR)
                 bank = ps2.tile([P, BANK], F32, name="bank2")
                 match(bank[:], mt, bq)
-                nc.vector.tensor_tensor(
-                    weighted[mt // 2][:, mt % 2, :], bank[:], pw[mt // 2][:, mt % 2, :], ALU.mult
-                )
+                nc.vector.tensor_tensor(weighted[pair][:, n, :], bank[:], pw[pair][:, n, :], ALU.mult)
 
         quantise_w(0, 0)
         plain_reading(0)
         plain_reading(1)
         quantise_w(1, 0)
-        gather_opening_words(0, 0)
-        gather_opening_scales(0)
-        gather_opening_words(1, 0)
-        gather_opening_words(0, 1)
-        gather_opening_scales(1, "w_bf10")
-        gather_opening_words(1, 1, "b_rows12")
+        gather_opening(0)
+        gather_opening(1, "b_bf0", "b_bf1")
         quantise_w(0, 1)
-        quantise_w(1, 1)
-        weigh(range(4))
-        carry_over(0, 0)
-        carry_over(0, 1)
-        carry_over(1, 0)
-        carry_over(1, 1)
-        weigh(range(4, 8))
+        quantise_w(1, 1, LAST_QUARTER_CUT)
+        weigh(0)
+        for rp in range(NP):
+            for jh in range(S // JH):
+                carry_over(rp, jh)
+        weigh(1)
 
         for jh in range(S // JH):
-            cols = slice(JH * jh, JH * (jh + 1))
-            for g in range(S2 // (2 * P)):
-                bank = ps2.tile([P, 2, JH], F32, name="bank2")
-                for n in range(2):
-                    match(bank[:, n, :], 2 * g + n, [hq[b, jh] for b in range(NP)])
-                last = jh == S // JH - 1 and g == S2 // (2 * P) - 1
-                step = 1 if last else 2
-                for lo in range(0, 2, step):
-                    tiles = slice(lo, lo + step)
+            jcols = slice(JH * jh, JH * (jh + 1))
+            for pair in range(S2 // (PAIR * P)):
+                bank = ps2.tile([P, PAIR, JH], F32, name="bank2")
+                for n in range(PAIR):
+                    match(bank[:, n, :], PAIR * pair + n, [hq[rp, jh] for rp in range(NP)])
+                last = jh == S // JH - 1 and pair == S2 // (PAIR * P) - 1
+                step = 1 if last else PAIR
+                for n in range(0, PAIR, step):
+                    tiles = slice(n, n + step)
                     diff = ring.tile([P, step, JH], F32, name="diff")
-                    nc.vector.tensor_tensor(diff[:], bank[:, tiles, :], weighted[g][:, tiles, cols], ALU.subtract)
+                    nc.vector.tensor_tensor(diff[:], bank[:, tiles, :], weighted[pair][:, tiles, jcols], ALU.subtract)
                     score = ring.tile([P, step, JH], F32, name="score")
                     nc.scalar.activation(out=score[:], in_=diff[:], func=ACT.Tanh)
-                    rows = slice(P * (2 * g + lo), P * (2 * g + lo + step))
-                    nc.sync.dma_start(out=out[rows, cols].rearrange("(n p) j -> p n j", p=P), in_=score[:])
+                    mrows = slice(P * (PAIR * pair + n), P * (PAIR * pair + n + step))
+                    nc.sync.dma_start(out=out[mrows, jcols].rearrange("(n p) j -> p n j", p=P), in_=score[:])

from contextlib import ExitStack

import concourse.mybir as mybir
from concourse.masks import make_identity

K, T, S, S2 = 1024, 2048, 512, 1024
FLOPS = 2 * K * K * S * 2 + 2 * K * S2 * S * 2

F32 = mybir.dt.float32
BF16 = mybir.dt.bfloat16
I32 = mybir.dt.int32
U32 = mybir.dt.uint32
U16 = mybir.dt.uint16
U8 = mybir.dt.uint8
FP8X4 = mybir.dt.float8_e4m3fn_x4
FP4X4 = mybir.dt.float4_e2m1fn_x4
ACT = mybir.ActivationFunctionType
ALU = mybir.AluOpType

P = 128
PACK = 4
KP = P * PACK
NP = K // KP
BANK = 512
QUADS = 4
SCALE_ROWS = 4
LIST_GROUP = 16
PART = 512
JH = S // 2
PAIR = 2
GAIN_RUN = K // P
LAST_QUARTER_CUT = P // 2
EPILOGUE_STEPS = (S // JH) * (S2 // (PAIR * P)) + 1


def tile_list_double_bill_carryover_kernel(
    tc, tab_words, tab_scales, offs, offs2, w, w4_words, w4_scales, gain, pairw, out
):
    nc = tc.nc
    with ExitStack() as ctx:
        keep = ctx.enter_context(tc.tile_pool(name="keep", bufs=1))
        ring = ctx.enter_context(tc.tile_pool(name="ring", bufs=EPILOGUE_STEPS))
        ps1 = ctx.enter_context(tc.psum_pool(name="ps1", bufs=4))
        ps2 = ctx.enter_context(tc.psum_pool(name="ps2", bufs=4))

        def held(shape, dtype, name, tag=None):
            return keep.tile(shape, dtype, name=name, tag=tag or name, align_bytes=64)

        idx = keep.tile([P, S // LIST_GROUP], U16, name="idx")
        idx2 = keep.tile([P, S2 // LIST_GROUP], U16, name="idx2")
        tabw = [held([P, T], I32, "tabw%d" % a) for a in range(NP)]
        tabs = held([P, T], U8, "tabs")
        w4w = held([P, NP, 2 * K], U8, "w4w")
        w4s = held([P, NP * K], U8, "w4s")
        gain_rows = held([P, GAIN_RUN], F32, "gain_rows")
        vs1 = held([P, S], U8, "vs1")
        ident = held([P, P], F32, "ident")

        nc.gpsimd.memset(tabs[:].bitcast(I32), 0)
        nc.vector.memset(w4s[:].bitcast(I32), 0)
        nc.vector.memset(vs1[:].bitcast(I32), 0)
        make_identity(nc, ident[:])

        def load_table_words(a, pieces):
            words = tab_words[a].rearrange("p t i -> p (t i)").bitcast(I32)
            for lo in range(0, T, T // pieces):
                nc.sync.dma_start(out=tabw[a][:, lo : lo + T // pieces], in_=words[:, lo : lo + T // pieces])

        def load_table_scales():
            for q in range(QUADS):
                nc.sync.dma_start(
                    out=tabs[32 * q : 32 * q + NP * SCALE_ROWS, :].bitcast(I32),
                    in_=tab_scales[:, SCALE_ROWS * q : SCALE_ROWS * (q + 1), :].bitcast(I32),
                )

        def load_w4_scales():
            for s in range(SCALE_ROWS):
                nc.sync.dma_start(
                    out=w4s[s:P:32, :].rearrange("q (a c) -> q a c", a=NP).bitcast(I32),
                    in_=w4_scales[:, s : QUADS * SCALE_ROWS : SCALE_ROWS, :].rearrange("a q c -> q a c").bitcast(I32),
                )

        w_raw = {}

        def load_w(a, rp):
            w_raw[a, rp] = held([P, PACK, KP], F32, "w_raw%d%d" % (a, rp))
            nc.sync.dma_start(
                out=w_raw[a, rp][:],
                in_=w[a * KP : (a + 1) * KP, rp * KP : (rp + 1) * KP].rearrange("(p i) c -> p i c", i=PACK),
            )

        pw = []

        def load_pairw(pair):
            pw.append(held([P, PAIR, S], F32, "pw%d" % pair))
            nc.sync.dma_start(
                out=pw[pair][:],
                in_=pairw[pair * PAIR * P : (pair + 1) * PAIR * P, :].rearrange("(n p) j -> p n j", p=P),
            )

        def gather(name, dtype, window, offsets, tag=None):
            got = held([P, PART], dtype, name, tag)
            nc.vector.tensor_copy(got[:], window.indirect(offsets))
            return got

        nc.sync.dma_start(idx[:], offs)
        load_table_words(0, 2)
        nc.sync.dma_start(out=gain_rows[:], in_=gain.rearrange("(p c) -> p c", c=GAIN_RUN))
        load_table_scales()
        nc.sync.dma_start(idx2[:], offs2)
        nc.sync.dma_start(out=w4w[:].bitcast(I32), in_=w4_words.rearrange("a p c -> p a c").bitcast(I32))
        load_table_words(1, 1)
        load_w4_scales()

        vw = [None, None]
        vw[0] = gather("vw0", U32, tabw[0][:].bitcast(U32), idx[:])
        vs = gather("vs", U8, tabs[:], idx[:])
        span = 32 * (QUADS - 1) + SCALE_ROWS
        nc.sync.dma_start(out=vs1[0:span, :].bitcast(I32), in_=vs[SCALE_ROWS : SCALE_ROWS + span, :].bitcast(I32))
        for rp in range(NP):
            for a in range(NP):
                load_w(a, rp)
        for pair in range(S2 // (PAIR * P)):
            load_pairw(pair)

        vw[1] = gather("vw1", U32, tabw[1][:].bitcast(U32), idx[:])

        gain_all = held([P, K], F32, "gain_all")
        for run in range(GAIN_RUN // PACK):
            bank = ps2.tile([P, PACK, P], F32, name="bank2")
            for c in range(PACK):
                col = PACK * run + c
                nc.tensor.transpose(bank[:, c, :], gain_rows[:, col : col + 1].to_broadcast([P, P]), ident[:])
            nc.scalar.copy(
                out=gain_all[:].rearrange("q (n h c) -> q h n c", h=GAIN_RUN // PACK, c=PACK)[:, run],
                in_=bank[:].rearrange("q c n -> q n c"),
            )

        def quantise(name, rounded, width):
            codes, scales = held([P, width], U32, name + "_codes"), held([P, width], U8, name + "_scales")
            nc.vector.quantize_mx(out=codes[:].bitcast(FP8X4), scales=scales[:], in_=rounded[:])
            return codes, scales

        wq = {}

        def quantise_w(a, rp, cut=P):
            rounded = held([P, PACK * KP], BF16, "w_bf%d%d" % (a, rp))
            dst = rounded[:].rearrange("p (t m i) -> p m i t", t=PACK, i=PACK)
            src = w_raw[a, rp][:].rearrange("p i (m t) -> p m i t", t=PACK)
            nc.scalar.copy(out=dst[:, :cut], in_=src[:, :cut])
            if cut < P:
                nc.vector.tensor_copy(out=dst[:, cut:], in_=src[:, cut:])
            wq[a, rp] = quantise("wq%d%d" % (a, rp), rounded, KP)

        bq = [None, None]

        def plain_reading(rp):
            b_rows = []
            for jt in range(S // P):
                jcols = slice(P * jt, P * (jt + 1))
                bank = ps1.tile([P, BANK], F32, name="bank1")
                for a in range(NP):
                    nc.tensor.matmul_mx(
                        out=bank[:],
                        lhsT=vw[a][:, jcols].bitcast(FP8X4),
                        lhsT_scale=(vs if a == 0 else vs1)[:, jcols],
                        rhs=w4w[:, a, 2 * KP * rp : 2 * KP * (rp + 1)].bitcast(FP4X4),
                        rhs_scale=w4s[:, K * a + KP * rp : K * a + KP * (rp + 1)],
                        start=(a == 0),
                        stop=(a == NP - 1),
                    )
                b_rows.append(held([P, KP], BF16, "b_rows%d%d" % (rp, jt)))
                nc.vector.tensor_tensor(b_rows[jt][:], bank[:], gain_all[:, KP * rp : KP * (rp + 1)], ALU.mult)
            rounded = held([P, PACK * S], BF16, "b_bf%d" % rp)
            for two in range(S // (2 * P)):
                bank = ps2.tile([P, 2, 2, P], F32, name="bank2")
                for n in range(2):
                    words = b_rows[2 * two + n][:].bitcast(F32)
                    for u in range(2):
                        nc.tensor.transpose(bank[:, n, u, :], words[:, u : KP // 2 : 2], ident[:])
                nc.scalar.copy(
                    out=rounded[:].bitcast(F32)[:, BANK * two : BANK * (two + 1)].rearrange(
                        "p (n j u) -> p n j u", n=2, u=2
                    ),
                    in_=bank[:].rearrange("p n u j -> p n j u"),
                )
            bq[rp] = quantise("bq%d" % rp, rounded, S)

        hq = {}

        def carry_over(rp, jh):
            rounded = held([P, PACK * JH], BF16, "h_bf%d%d" % (rp, jh))
            for jt in range(JH // P):
                jcols = slice(JH * jh + P * jt, JH * jh + P * (jt + 1))
                bank = ps1.tile([P, BANK], F32, name="bank1")
                for t in range(PACK):
                    for a in range(NP):
                        nc.tensor.matmul_mx(
                            out=bank[:, P * t : P * (t + 1)],
                            lhsT=wq[a, rp][0][:, P * t : P * (t + 1)].bitcast(FP8X4),
                            lhsT_scale=wq[a, rp][1][:, P * t : P * (t + 1)],
                            rhs=vw[a][:, jcols].bitcast(FP8X4),
                            rhs_scale=vs[SCALE_ROWS * a : P, jcols],
                            start=(a == 0),
                            stop=(a == NP - 1),
                        )
                nc.scalar.activation(
                    out=rounded[:, BANK * jt : BANK * (jt + 1)].rearrange("p (j t) -> p j t", t=PACK),
                    in_=bank[:].rearrange("p (t j) -> p j t", t=PACK),
                    func=ACT.Abs,
                )
            hq[rp, jh] = quantise("hq%d%d" % (rp, jh), rounded, JH)

        v2w, v2s = {}, {}

        def gather_opening(part, scales_tag=None, last_words_tag=None):
            offsets = idx2[:, part * (PART // LIST_GROUP) : (part + 1) * (PART // LIST_GROUP)]
            v2w[0, part] = gather("v2w0%d" % part, U32, tabw[0][:].bitcast(U32), offsets)
            v2s[part] = gather("v2s%d" % part, U8, tabs[:], offsets, scales_tag)
            v2w[1, part] = gather("v2w1%d" % part, U32, tabw[1][:].bitcast(U32), offsets, last_words_tag)

        def match(target, mt, operand):
            part, lo = divmod(P * mt, PART)
            for rp in range(NP):
                nc.tensor.matmul_mx(
                    out=target,
                    lhsT=v2w[rp, part][:, lo : lo + P].bitcast(FP8X4),
                    lhsT_scale=v2s[part][SCALE_ROWS * rp : P, lo : lo + P],
                    rhs=operand[rp][0][:].bitcast(FP8X4),
                    rhs_scale=operand[rp][1][:],
                    start=(rp == 0),
                    stop=(rp == NP - 1),
                )

        weighted = [held([P, PAIR, S], F32, "weighted%d" % pair) for pair in range(S2 // (PAIR * P))]

        def weigh(part):
            for mt in range(part * PART // P, (part + 1) * PART // P):
                pair, n = divmod(mt, PAIR)
                bank = ps2.tile([P, BANK], F32, name="bank2")
                match(bank[:], mt, bq)
                nc.vector.tensor_tensor(weighted[pair][:, n, :], bank[:], pw[pair][:, n, :], ALU.mult)

        quantise_w(0, 0)
        plain_reading(0)
        plain_reading(1)
        quantise_w(1, 0)
        gather_opening(0)
        gather_opening(1, "b_bf0", "b_bf1")
        quantise_w(0, 1)
        quantise_w(1, 1, LAST_QUARTER_CUT)
        weigh(0)
        for rp in range(NP):
            for jh in range(S // JH):
                carry_over(rp, jh)
        weigh(1)

        for jh in range(S // JH):
            jcols = slice(JH * jh, JH * (jh + 1))
            for pair in range(S2 // (PAIR * P)):
                bank = ps2.tile([P, PAIR, JH], F32, name="bank2")
                for n in range(PAIR):
                    match(bank[:, n, :], PAIR * pair + n, [hq[rp, jh] for rp in range(NP)])
                last = jh == S // JH - 1 and pair == S2 // (PAIR * P) - 1
                step = 1 if last else PAIR
                for n in range(0, PAIR, step):
                    tiles = slice(n, n + step)
                    diff = ring.tile([P, step, JH], F32, name="diff")
                    nc.vector.tensor_tensor(diff[:], bank[:, tiles, :], weighted[pair][:, tiles, jcols], ALU.subtract)
                    score = ring.tile([P, step, JH], F32, name="score")
                    nc.scalar.activation(out=score[:], in_=diff[:], func=ACT.Tanh)
                    mrows = slice(P * (PAIR * pair + n), P * (PAIR * pair + n + step))
                    nc.sync.dma_start(out=out[mrows, jcols].rearrange("(n p) j -> p n j", p=P), in_=score[:])
